import numpy as np
import ml_dtypes


def mxq(x, axis, fmt="e4m3"):
    dtype, down = {"e4m3": (ml_dtypes.float8_e4m3fn, 7), "e5m2": (ml_dtypes.float8_e5m2, 14)}[fmt]
    v = np.moveaxis(np.asarray(x, np.float32).astype(ml_dtypes.bfloat16).astype(np.float64), axis, -1)
    blocks = v.reshape(v.shape[:-1] + (-1, 32))
    amax = np.abs(blocks).max(-1, keepdims=True)
    byte = np.maximum(np.where(amax > 0, np.frexp(amax)[1] - 1 + 127, 0) - down, 1)
    scale = np.exp2(byte - 127.0)
    codes = (blocks / scale).astype(np.float32).astype(dtype).astype(np.float64)
    return np.moveaxis((codes * scale).reshape(v.shape), -1, axis)


WIDE = False


def mx_kscale(k):
    if not WIDE:
        return np.ones(k)
    levels = np.array([10, -10, 5, -5, 0])
    if k % 512:
        return np.exp2(np.random.permutation(np.resize(levels, k // 32))).repeat(32)
    a = np.empty((k // 512, 16))
    for p in range(k // 512):
        a[p, :8] = np.random.permutation(np.resize(levels, 8))
        for g in range(8):
            far = levels[np.abs(levels - a[p, g]) >= 10]
            a[p, g + 8] = far[np.random.randint(len(far))]
    return np.exp2(a.ravel()).repeat(32)


def f64(x):
    return np.asarray(x).astype(np.float64)


def striped(idx):
    return np.tile(idx.reshape(-1, 16).T, (8, 1)).astype(np.uint16)


def unstriped(offs):
    return offs[:16].T.reshape(-1).astype(np.int64)


E2M1 = np.array([0.0, 0.5, 1.0, 1.5, 2.0, 3.0, 4.0, 6.0, -0.0, -0.5, -1.0, -1.5, -2.0, -3.0, -4.0, -6.0])


def pack_weight(w, fmt):
    k, n = w.shape
    w = f64(np.asarray(w, np.float32).astype(ml_dtypes.bfloat16)).reshape(k // 32, 32, n)
    amax = np.abs(w).max(1)
    if fmt == "e4m3":
        byte = np.frexp(amax)[1] - 1 + 127 - 7
    else:
        mant, ex = np.frexp(amax / 6.0)
        byte = np.where(mant > 0.5, ex, ex - 1) + 127
    byte = np.clip(np.where(amax > 0, byte, 1), 1, 254)
    scaled = (w * np.exp2(127.0 - byte)[:, None, :]).reshape(k, n).astype(np.float32)
    by_word = np.ascontiguousarray(scaled.reshape(k // 512, 128, 4, n).transpose(0, 1, 3, 2))
    if fmt == "e4m3":
        words = by_word.astype(ml_dtypes.float8_e4m3fn).view(np.uint8)
    else:
        c = by_word.astype(ml_dtypes.float4_e2m1fn).view(np.uint8) & 0xF
        words = (c[..., 0::2] | (c[..., 1::2] << 4)).reshape(k // 512, 128, 2 * n)
    return np.ascontiguousarray(words), np.ascontiguousarray(byte.astype(np.uint8).reshape(k // 512, 16, n))


def unpack_weight(words, scales, fmt):
    g, _, n = scales.shape
    words = np.ascontiguousarray(words).reshape(g, 128, n, -1)
    if fmt == "e4m3":
        vals = words.view(ml_dtypes.float8_e4m3fn).astype(np.float64)
    else:
        nib = np.empty((g, 128, n, 4), np.uint8)
        nib[..., 0::2] = words & 0xF
        nib[..., 1::2] = words >> 4
        vals = E2M1[nib]
    vals = vals * np.repeat(np.exp2(scales.astype(np.float64) - 127.0), 8, axis=1)[..., None]
    return vals.transpose(0, 1, 3, 2).reshape(g * 512, n)


def gelu(v):
    return 0.5 * v * (1.0 + np.tanh(np.sqrt(2.0 / np.pi) * (v + 0.044715 * v**3)))


K, K2, T, T3, S, T2, H, N = 1024, 512, 2048, 1024, 512, 1024, 1024, 512

def setup_inputs():
    n = np.random.standard_normal
    s, s2, u = mx_kscale(K)[:, None], mx_kscale(K2)[:, None], mx_kscale(H)[:, None]
    tab_words, tab_scales = pack_weight(n((K, T)) * s, "e4m3")
    tab2_words, tab2_scales = pack_weight(n((K2, T3)) * s2, "e4m3")
    w2_words, w2_scales = pack_weight(1.8 * n((K2, H)) / np.sqrt(K2) / s2, "e2m1")
    w4_words, w4_scales = pack_weight(n((H, N)) / np.sqrt(H) / u, "e2m1")
    return {
        "tab_words": tab_words, "tab_scales": tab_scales,
        "tab2_words": tab2_words, "tab2_scales": tab2_scales,
        "offs": striped(np.random.permutation(T)[:S]),
        "offs2": striped(np.random.permutation(T3)[:S]),
        "offs3": striped(np.random.permutation(T2)[:S]),
        "offs4": striped(np.random.permutation(T2)[:S]),
        "w1": (1.5 * n((K, H)) / np.sqrt(K) / s).astype(np.float32),
        "b1": (0.6 * n(H)).astype(np.float32),
        "gn1": (np.random.uniform(0.8, 1.8, H) * u[:, 0]).astype(np.float32),
        "w2_words": w2_words, "w2_scales": w2_scales,
        "gn2": (np.random.uniform(0.6, 1.4, H) * u[:, 0]).astype(np.float32),
        "wg1": np.exp(0.3 * n((128, S))).astype(np.float32),
        "wg2": np.exp(0.3 * n((128, S))).astype(np.float32),
        "tide": (0.7 * n((H, T2)) * u).astype(np.float32),
        "w3": (1.5 * n((H, N)) / np.sqrt(H) / u).astype(np.float32),
        "w4_words": w4_words, "w4_scales": w4_scales,
    }

def reference(tab_words, tab_scales, tab2_words, tab2_scales, offs, offs2, offs3, offs4, w1, b1, gn1,
              w2_words, w2_scales, gn2, wg1, wg2, tide, w3, w4_words, w4_scales):
    v = unpack_weight(tab_words, tab_scales, "e4m3")[:, unstriped(offs)]
    v2 = unpack_weight(tab2_words, tab2_scales, "e4m3")[:, unstriped(offs2)]
    h1 = np.tanh((mxq(f64(w1), 0, "e4m3").T @ v) + f64(b1)[:, None]) * f64(gn1)[:, None]
    a2 = unpack_weight(w2_words, w2_scales, "e2m1").T @ v2
    h2 = a2 / (1.0 + np.exp(-a2)) * f64(gn2)[:, None]
    pa = np.zeros((H, T2))
    pa[:, unstriped(offs3)] = np.tile(f64(wg1), (H // 128, 1)) * h1
    pb = np.zeros((H, T2))
    pb[:, unstriped(offs4)] = np.tile(f64(wg2), (H // 128, 1)) * h2
    z = np.maximum(np.maximum(pa, pb), f64(tide))
    zq = mxq(z, 0, "e4m3")
    y1 = mxq(f64(w3), 0, "e4m3").T @ zq
    y2 = unpack_weight(w4_words, w4_scales, "e2m1").T @ zq
    return np.tanh(y1) + y2

@@ -1,0 +1,348 @@
+from contextlib import ExitStack
+
+import concourse.mybir as mybir
+
+K, K2, T, T3, S, T2, H, N = 1024, 512, 2048, 1024, 512, 1024, 1024, 512
+FLOPS = 2 * (K * H * S + K2 * H * S + 2 * H * N * T2)
+
+F32 = mybir.dt.float32
+BF16 = mybir.dt.bfloat16
+I32 = mybir.dt.int32
+U32 = mybir.dt.uint32
+U16 = mybir.dt.uint16
+U8 = mybir.dt.uint8
+FP8X4 = mybir.dt.float8_e4m3fn_x4
+FP4X4 = mybir.dt.float4_e2m1fn_x4
+ACT = mybir.ActivationFunctionType
+ALU = mybir.AluOpType
+
+P = 128
+PACK = 4
+KP = P * PACK
+SLICES = H // P
+HALF = 512
+QUARTER = 256
+PB_PAGES = 4
+PA_PAGES = 3
+
+
+def tile_list_tsunami_alert_scores_kernel(
+    tc, tab_words, tab_scales, tab2_words, tab2_scales, offs, offs2, offs3, offs4, w1, b1, gn1,
+    w2_words, w2_scales, gn2, wg1, wg2, tide, w3, w4_words, w4_scales, out,
+):
+    nc = tc.nc
+    with ExitStack() as ctx:
+        keep = ctx.enter_context(tc.tile_pool(name="keep", bufs=1))
+        ring = ctx.enter_context(tc.tile_pool(name="ring", bufs=4))
+        rows = ctx.enter_context(tc.tile_pool(name="rows", bufs=10))
+        psum = ctx.enter_context(tc.psum_pool(name="psum", bufs=1))
+
+        def held(name, shape, dtype):
+            return keep.tile(shape, dtype, name=name, align_bytes=64)
+
+        def bank(i):
+            return psum.tile([P, HALF], F32, name="bank%d" % i)
+
+        def load(dst, src):
+            nc.sync.dma_start(out=dst, in_=src)
+
+        def load_list(name, src):
+            lst = keep.tile([P, S // 16], U16, name=name)
+            nc.sync.dma_start(lst[:], src)
+            return lst
+
+        def zero_plane(name, width):
+            plane = held(name, [P, width], U8)
+            nc.vector.memset(plane[:].bitcast(I32), 0)
+            return plane
+
+        def load_dealt(name, wg):
+            dealt = held(name, [P, PACK, S], F32)
+            for u in range(4):
+                load(dealt[32 * u : 32 * u + 32], wg.rearrange("(q t) j -> q t j", t=PACK))
+            return dealt
+
+        def load_channels(name, vec):
+            col = held(name, [P, 2, PACK], F32)
+            load(col[:], vec.rearrange("(b p t) -> p b t", b=2, t=PACK))
+            return col
+
+        tab2_plane = zero_plane("tab2_plane", T3)
+        w2_plane_raw = zero_plane("w2_plane_raw", H)
+        tab_plane = zero_plane("tab_plane", T)
+        w4_plane = zero_plane("w4_plane", 2 * N)
+        pb_pages = [held("pb%d" % i, [P, T2], F32) for i in range(PB_PAGES)]
+        pa_pages = [held("pa%d" % i, [P, T2], F32) for i in range(PA_PAGES)]
+        for page in pb_pages[:2]:
+            nc.vector.memset(page[:], 0.0)
+        for page in pb_pages[2:] + pa_pages:
+            nc.gpsimd.memset(page[:], 0.0)
+
+        list2 = load_list("list2", offs2)
+        tab2_sb = held("tab2_sb", [P, T3], I32)
+        load(tab2_sb[:], tab2_words[0].rearrange("p t i -> p (t i)").bitcast(I32))
+        for q in range(4):
+            load(tab2_plane[32 * q : 32 * q + 4, :].bitcast(I32), tab2_scales[0, 4 * q : 4 * q + 4, :].bitcast(I32))
+        w2_raw = held("w2_raw", [P, 2 * H], U8)
+        load(w2_raw[:].bitcast(I32), w2_words[0].bitcast(I32))
+        for q in range(4):
+            load(w2_plane_raw[32 * q : 32 * q + 4, :].bitcast(I32), w2_scales[0, 4 * q : 4 * q + 4, :].bitcast(I32))
+        list4 = load_list("list4", offs4)
+        wg2_sb = load_dealt("wg2_sb", wg2)
+        gn2_sb = load_channels("gn2_sb", gn2)
+
+        tide_rows = tide.rearrange("(b p t) m -> b t p m", b=2, t=PACK)
+        tide_sb = [held("tide%d" % s, [P, T2], F32) for s in range(SLICES)]
+
+        def load_tide(s):
+            load(tide_sb[s][:], tide_rows[s // PACK, s % PACK])
+
+        def load_weight(w, a, cols):
+            raw = ring.tile([P, PACK, HALF], F32, name="raw")
+            load(raw[:], w[KP * a : KP * (a + 1), cols].rearrange("(p j) c -> p j c", j=PACK))
+            return raw
+
+        load_tide(0)
+        load_tide(1)
+        list1 = load_list("list1", offs)
+        tab_sb = [held("tab_sb%d" % a, [P, T], I32) for a in range(2)]
+        for a in range(2):
+            load(tab_sb[a][:], tab_words[a].rearrange("p t i -> p (t i)").bitcast(I32))
+        for q in range(4):
+            load(tab_plane[32 * q : 32 * q + 8, :].bitcast(I32), tab_scales[:, 4 * q : 4 * q + 4, :].bitcast(I32))
+        b1_sb = load_channels("b1_sb", b1)
+        gn1_sb = load_channels("gn1_sb", gn1)
+        w1_raw = {}
+        load_tide(2)
+        w1_raw[0, 0] = load_weight(w1, 0, slice(0, HALF))
+        load_tide(3)
+        w1_raw[1, 0] = load_weight(w1, 1, slice(0, HALF))
+        load_tide(4)
+        load_tide(5)
+        w1_raw[0, 1] = load_weight(w1, 0, slice(HALF, H))
+        load_tide(6)
+        w1_raw[1, 1] = load_weight(w1, 1, slice(HALF, H))
+        list3 = load_list("list3", offs3)
+        wg1_sb = load_dealt("wg1_sb", wg1)
+        load_tide(7)
+        w4_sb = held("w4_sb", [P, 2, 2 * N], U8)
+        load(w4_sb[:].bitcast(I32), w4_words.rearrange("a p c -> p a c").bitcast(I32))
+        for q in range(4):
+            load(
+                w4_plane[32 * q : 32 * q + 4, :].bitcast(I32).rearrange("r (a c) -> r a c", a=2),
+                w4_scales[:, 4 * q : 4 * q + 4, :].rearrange("a r c -> r a c").bitcast(I32),
+            )
+
+        v2_words = held("v2_words", [P, S], U32)
+        v2_plane = held("v2_plane", [P, S], U8)
+        nc.vector.tensor_copy(v2_words[:], tab2_sb[:].bitcast(U32).indirect(list2[:]))
+        nc.vector.tensor_copy(v2_plane[:], tab2_plane[:].indirect(list2[:]))
+        w2_sb = held("w2_sb", [P, 2 * H], U8)
+        w2_plane = held("w2_plane", [P, H], U8)
+        nc.vector.tensor_copy(
+            out=w2_sb[:].bitcast(U16).rearrange("p (b t q) -> p b t q", b=2, t=PACK),
+            in_=w2_raw[:].bitcast(U16).rearrange("p (b q t) -> p b t q", b=2, t=PACK),
+        )
+        nc.vector.tensor_copy(
+            out=w2_plane[:].rearrange("p (b t q) -> p b t q", b=2, t=PACK),
+            in_=w2_plane_raw[:].rearrange("p (b q t) -> p b t q", b=2, t=PACK),
+        )
+        h2 = []
+        for s in range(SLICES):
+            acc = bank(s)
+            nc.tensor.matmul_mx(
+                out=acc[:],
+                lhsT=w2_sb[:, 2 * P * s : 2 * P * (s + 1)].bitcast(FP4X4),
+                lhsT_scale=w2_plane[:, P * s : P * (s + 1)],
+                rhs=v2_words[:].bitcast(FP8X4),
+                rhs_scale=v2_plane[:],
+                start=True,
+                stop=True,
+            )
+            h = rows.tile([P, S], F32, name="row")
+            nc.scalar.activation(out=h[:], in_=acc[:], func=ACT.Silu)
+            h2.append(h)
+
+        def scatter_b(s):
+            page = pb_pages[s % PB_PAGES]
+            nc.vector.tensor_tensor(page[:].indirect(list4[:]), h2[s][:], wg2_sb[:, s % PACK, :], ALU.mult)
+
+        def max_b(s):
+            nc.vector.scalar_tensor_tensor(
+                out=tide_sb[s][:], in0=pb_pages[s % PB_PAGES][:], scalar=gn2_sb[:, s // PACK, s % PACK : s % PACK + 1],
+                in1=tide_sb[s][:], op0=ALU.mult, op1=ALU.max,
+            )
+
+        v_words = [held("v_words%d" % a, [P, S], U32) for a in range(2)]
+        v_plane = held("v_plane", [P, S], U8)
+
+        def gather_records():
+            for a in range(2):
+                nc.vector.tensor_copy(v_words[a][:], tab_sb[a][:].bitcast(U32).indirect(list1[:]))
+            nc.vector.tensor_copy(v_plane[:], tab_plane[:].indirect(list1[:]))
+
+        def quantize(name, staged):
+            codes = held(name + "_codes", [P, HALF], U32)
+            plane = held(name + "_plane", [P, HALF], U8)
+            nc.vector.quantize_mx(out=codes[:].bitcast(FP8X4), scales=plane[:], in_=staged[:])
+            return codes, plane
+
+        def stage_tile():
+            return ring.tile([P, PACK * HALF], BF16, name="staged", align_bytes=64)
+
+        w1_staged = {}
+        w1_q = {}
+
+        def cast_w1(a, b):
+            staged = stage_tile()
+            nc.scalar.copy(
+                out=staged[:].rearrange("p (t m j) -> p m j t", t=PACK, j=PACK),
+                in_=w1_raw[a, b][:].rearrange("p j (m t) -> p m j t", t=PACK),
+            )
+            w1_staged[a, b] = staged
+
+        def quantize_w1(a, b):
+            w1_q[a, b] = quantize("w1_%d%d" % (a, b), w1_staged[a, b])
+
+        h1 = []
+
+        def first_product_a(b):
+            for t in range(PACK):
+                acc = bank(PACK * b + t)
+                for a in range(2):
+                    codes, plane = w1_q[a, b]
+                    nc.tensor.matmul_mx(
+                        out=acc[:],
+                        lhsT=codes[:, P * t : P * (t + 1)].bitcast(FP8X4),
+                        lhsT_scale=plane[:, P * t : P * (t + 1)],
+                        rhs=v_words[a][:].bitcast(FP8X4),
+                        rhs_scale=v_plane[4 * a :, :],
+                        start=(a == 0),
+                        stop=(a == 1),
+                    )
+                h = rows.tile([P, S], F32, name="row")
+                nc.scalar.activation(out=h[:], in_=acc[:], func=ACT.Tanh, bias=b1_sb[:, b, t : t + 1])
+                h1.append(h)
+
+        w3_q = {}
+        w3_staged = {}
+
+        def cast_w3(a):
+            raw = load_weight(w3, a, slice(0, N))
+            staged = stage_tile()
+            nc.scalar.copy(
+                out=staged[:].rearrange("p (c i j) -> p c j i", i=4, j=PACK),
+                in_=raw[:].rearrange("p j (c i) -> p c j i", i=4),
+            )
+            w3_staged[a] = staged
+
+        scatter_b(0)
+        scatter_b(1)
+        max_b(0)
+        gather_records()
+        for a, b in ((0, 0), (1, 0), (0, 1), (1, 1)):
+            cast_w1(a, b)
+        for s in range(2, SLICES):
+            scatter_b(s)
+            max_b(s - 1)
+            if s == 3:
+                quantize_w1(0, 0)
+                quantize_w1(1, 0)
+                first_product_a(0)
+            if s == 5:
+                quantize_w1(0, 1)
+                quantize_w1(1, 1)
+                first_product_a(1)
+        for a in range(2):
+            cast_w3(a)
+
+        z = [held("z%d" % b, [P, 4, PACK, QUARTER], BF16) for b in range(2)]
+
+        def scatter_a(s):
+            page = pa_pages[s % PA_PAGES]
+            nc.vector.tensor_tensor(page[:].indirect(list3[:]), h1[s][:], wg1_sb[:, s % PACK, :], ALU.mult)
+
+        def max_a(s, q0=0, q1=4):
+            cols = slice(QUARTER * q0, QUARTER * q1)
+            nc.vector.scalar_tensor_tensor(
+                out=z[s // PACK][:, q0:q1, s % PACK, :],
+                in0=pa_pages[s % PA_PAGES][:, cols].rearrange("p (q c) -> p q c", c=QUARTER),
+                scalar=gn1_sb[:, s // PACK, s % PACK : s % PACK + 1],
+                in1=tide_sb[s][:, cols].rearrange("p (q c) -> p q c", c=QUARTER),
+                op0=ALU.mult, op1=ALU.max,
+            )
+
+        z_staged = {}
+        z_q = {}
+
+        def interleave(b, q, on_vector):
+            if q % 2 == 0:
+                z_staged[b, q // 2] = stage_tile()
+            dst = z_staged[b, q // 2][:, (q % 2) * PACK * QUARTER : (q % 2 + 1) * PACK * QUARTER]
+            dst = dst.rearrange("p (c i t) -> p c t i", i=4, t=PACK)
+            src = z[b][:, q, :, :].rearrange("p t (c i) -> p c t i", i=4)
+            if on_vector:
+                nc.vector.tensor_copy(out=dst, in_=src)
+            else:
+                nc.scalar.copy(out=dst, in_=src)
+
+        def quantize_z(b, half):
+            z_q[b, half] = quantize("z_%d%d" % (b, half), z_staged[b, half])
+
+        def read_out_pass(acc, which, n, b, half):
+            codes, plane = z_q[b, half]
+            if which == 0:
+                w_codes = w3_q[b][0][:, P * n : P * (n + 1)].bitcast(FP8X4)
+                w_plane = w3_q[b][1][:, P * n : P * (n + 1)]
+            else:
+                w_codes = w4_sb[:, b, 2 * P * n : 2 * P * (n + 1)].bitcast(FP4X4)
+                w_plane = w4_plane[:, N * b + P * n : N * b + P * (n + 1)]
+            nc.tensor.matmul_mx(
+                out=acc[:], lhsT=w_codes, lhsT_scale=w_plane, rhs=codes[:].bitcast(FP8X4), rhs_scale=plane[:],
+                start=(b == 0), stop=(b == 1),
+            )
+
+        def finish(y1, y2, n, half):
+            res = rows.tile([P, HALF], F32, name="row")
+            nc.scalar.activation(out=res[:], in_=y1[:], func=ACT.Tanh)
+            nc.vector.tensor_tensor(res[:], y2[:], res[:], ALU.add)
+            nc.sync.dma_start(out=out[P * n : P * (n + 1), HALF * half : HALF * (half + 1)], in_=res[:])
+
+        scatter_a(0)
+        max_b(SLICES - 1)
+        for s in range(1, SLICES):
+            scatter_a(s)
+            max_a(s - 1)
+            if s == 2:
+                for a in range(2):
+                    w3_q[a] = quantize("w3_%d" % a, w3_staged[a])
+            if s == PACK:
+                for q in range(4):
+                    interleave(0, q, False)
+        last = SLICES - 1
+        quantize_z(0, 0)
+        sums = [[bank(2 * n + which) for which in range(2)] for n in range(N // P)]
+        for n in range(N // P):
+            for which in range(2):
+                read_out_pass(sums[n][which], which, n, 0, 0)
+        max_a(last, 0, 1)
+        interleave(1, 0, False)
+        max_a(last, 1, 2)
+        max_a(last, 2, 4)
+        interleave(1, 1, True)
+        interleave(1, 2, False)
+        quantize_z(0, 1)
+        quantize_z(1, 0)
+        interleave(1, 3, True)
+        for n in range(N // P):
+            for which in range(2):
+                read_out_pass(sums[n][which], which, n, 1, 0)
+        quantize_z(1, 1)
+        for n in range(N // P):
+            finish(sums[n][0], sums[n][1], n, 0)
+        for n in range(N // P):
+            pair = [bank(2 * n + which) for which in range(2)]
+            for which in range(2):
+                for b in range(2):
+                    read_out_pass(pair[which], which, n, b, 1)
+            finish(pair[0], pair[1], n, 1)

@@ -22,7 +22,7 @@ KP = P * PACK
 SLICES = H // P
 HALF = 512
 QUARTER = 256
-PB_PAGES = 4
+PB_PAGES = 3
 PA_PAGES = 3
 
 
@@ -37,8 +37,8 @@ def tile_list_tsunami_alert_scores_kernel(
         rows = ctx.enter_context(tc.tile_pool(name="rows", bufs=10))
         psum = ctx.enter_context(tc.psum_pool(name="psum", bufs=1))
 
-        def held(name, shape, dtype):
-            return keep.tile(shape, dtype, name=name, align_bytes=64)
+        def held(name, shape, dtype, tag=""):
+            return keep.tile(shape, dtype, name=name, tag=tag, align_bytes=64)
 
         def bank(i):
             return psum.tile([P, HALF], F32, name="bank%d" % i)
@@ -51,10 +51,9 @@ def tile_list_tsunami_alert_scores_kernel(
             nc.sync.dma_start(lst[:], src)
             return lst
 
-        def zero_plane(name, width):
-            plane = held(name, [P, width], U8)
-            nc.vector.memset(plane[:].bitcast(I32), 0)
-            return plane
+        def load_plane(plane, scales, quadrants):
+            for q in quadrants:
+                load(plane[32 * q : 32 * q + 4, :].bitcast(I32), scales[0, 4 * q : 4 * q + 4, :].bitcast(I32))
 
         def load_dealt(name, wg):
             dealt = held(name, [P, PACK, S], F32)
@@ -67,26 +66,25 @@ def tile_list_tsunami_alert_scores_kernel(
             load(col[:], vec.rearrange("(b p t) -> p b t", b=2, t=PACK))
             return col
 
-        tab2_plane = zero_plane("tab2_plane", T3)
-        w2_plane_raw = zero_plane("w2_plane_raw", H)
-        tab_plane = zero_plane("tab_plane", T)
-        w4_plane = zero_plane("w4_plane", 2 * N)
+        tab2_plane = held("tab2_plane", [P, T3], U8, tag="tab2_plane")
+        w2_plane_raw = held("w2_plane_raw", [P, H], U8, tag="w2_plane_raw")
+        tab_plane = held("tab_plane", [P, T], U8)
+        w4_plane = held("w4_plane", [P, 2 * N], U8)
         pb_pages = [held("pb%d" % i, [P, T2], F32) for i in range(PB_PAGES)]
-        pa_pages = [held("pa%d" % i, [P, T2], F32) for i in range(PA_PAGES)]
-        for page in pb_pages[:2]:
-            nc.vector.memset(page[:], 0.0)
-        for page in pb_pages[2:] + pa_pages:
-            nc.gpsimd.memset(page[:], 0.0)
+        pa_pages = [held("pa0", [P, T2], F32)]
+        for plane in (tab2_plane, w2_plane_raw, tab_plane, w4_plane):
+            nc.gpsimd.memset(plane[:].bitcast(I32), 0)
+        for page in pb_pages + pa_pages:
+            nc.vector.memset(page[:].bitcast(I32), 0)
 
         list2 = load_list("list2", offs2)
-        tab2_sb = held("tab2_sb", [P, T3], I32)
-        load(tab2_sb[:], tab2_words[0].rearrange("p t i -> p (t i)").bitcast(I32))
-        for q in range(4):
-            load(tab2_plane[32 * q : 32 * q + 4, :].bitcast(I32), tab2_scales[0, 4 * q : 4 * q + 4, :].bitcast(I32))
-        w2_raw = held("w2_raw", [P, 2 * H], U8)
+        load_plane(tab2_plane, tab2_scales, (0, 1))
+        w2_raw = held("w2_raw", [P, 2 * H], U8, tag="w2_raw")
         load(w2_raw[:].bitcast(I32), w2_words[0].bitcast(I32))
-        for q in range(4):
-            load(w2_plane_raw[32 * q : 32 * q + 4, :].bitcast(I32), w2_scales[0, 4 * q : 4 * q + 4, :].bitcast(I32))
+        tab2_sb = held("tab2_sb", [P, T3], I32, tag="tab2_sb")
+        load(tab2_sb[:], tab2_words[0].rearrange("p t i -> p (t i)").bitcast(I32))
+        load_plane(tab2_plane, tab2_scales, (2, 3))
+        load_plane(w2_plane_raw, w2_scales, range(4))
         list4 = load_list("list4", offs4)
         wg2_sb = load_dealt("wg2_sb", wg2)
         gn2_sb = load_channels("gn2_sb", gn2)
@@ -102,36 +100,33 @@ def tile_list_tsunami_alert_scores_kernel(
             load(raw[:], w[KP * a : KP * (a + 1), cols].rearrange("(p j) c -> p j c", j=PACK))
             return raw
 
-        load_tide(0)
-        load_tide(1)
-        list1 = load_list("list1", offs)
-        tab_sb = [held("tab_sb%d" % a, [P, T], I32) for a in range(2)]
-        for a in range(2):
-            load(tab_sb[a][:], tab_words[a].rearrange("p t i -> p (t i)").bitcast(I32))
-        for q in range(4):
-            load(tab_plane[32 * q : 32 * q + 8, :].bitcast(I32), tab_scales[:, 4 * q : 4 * q + 4, :].bitcast(I32))
+        for s in range(5):
+            load_tide(s)
         b1_sb = load_channels("b1_sb", b1)
         gn1_sb = load_channels("gn1_sb", gn1)
         w1_raw = {}
-        load_tide(2)
         w1_raw[0, 0] = load_weight(w1, 0, slice(0, HALF))
-        load_tide(3)
         w1_raw[1, 0] = load_weight(w1, 1, slice(0, HALF))
-        load_tide(4)
-        load_tide(5)
         w1_raw[0, 1] = load_weight(w1, 0, slice(HALF, H))
-        load_tide(6)
         w1_raw[1, 1] = load_weight(w1, 1, slice(HALF, H))
-        list3 = load_list("list3", offs3)
-        wg1_sb = load_dealt("wg1_sb", wg1)
-        load_tide(7)
-        w4_sb = held("w4_sb", [P, 2, 2 * N], U8)
-        load(w4_sb[:].bitcast(I32), w4_words.rearrange("a p c -> p a c").bitcast(I32))
+        w3_raw = [load_weight(w3, a, slice(0, N)) for a in range(2)]
         for q in range(4):
             load(
                 w4_plane[32 * q : 32 * q + 4, :].bitcast(I32).rearrange("r (a c) -> r a c", a=2),
                 w4_scales[:, 4 * q : 4 * q + 4, :].rearrange("a r c -> r a c").bitcast(I32),
             )
+        w4_sb = held("w4_sb", [P, 2, 2 * N], U8)
+        load(w4_sb[:].bitcast(I32), w4_words.rearrange("a p c -> p a c").bitcast(I32))
+        list1 = load_list("list1", offs)
+        for q in range(4):
+            load(tab_plane[32 * q : 32 * q + 8, :].bitcast(I32), tab_scales[:, 4 * q : 4 * q + 4, :].bitcast(I32))
+        tab_sb = [held("tab_sb%d" % a, [P, T], I32) for a in range(2)]
+        for a in range(2):
+            load(tab_sb[a][:], tab_words[a].rearrange("p t i -> p (t i)").bitcast(I32))
+        for s in range(5, SLICES):
+            load_tide(s)
+        list3 = load_list("list3", offs3)
+        wg1_sb = load_dealt("wg1_sb", wg1)
 
         v2_words = held("v2_words", [P, S], U32)
         v2_plane = held("v2_plane", [P, S], U8)
@@ -139,16 +134,20 @@ def tile_list_tsunami_alert_scores_kernel(
         nc.vector.tensor_copy(v2_plane[:], tab2_plane[:].indirect(list2[:]))
         w2_sb = held("w2_sb", [P, 2 * H], U8)
         w2_plane = held("w2_plane", [P, H], U8)
-        nc.vector.tensor_copy(
-            out=w2_sb[:].bitcast(U16).rearrange("p (b t q) -> p b t q", b=2, t=PACK),
-            in_=w2_raw[:].bitcast(U16).rearrange("p (b q t) -> p b t q", b=2, t=PACK),
-        )
-        nc.vector.tensor_copy(
-            out=w2_plane[:].rearrange("p (b t q) -> p b t q", b=2, t=PACK),
-            in_=w2_plane_raw[:].rearrange("p (b q t) -> p b t q", b=2, t=PACK),
-        )
+
+        def deal_w2(b):
+            nc.vector.tensor_copy(
+                out=w2_sb[:, H * b : H * (b + 1)].bitcast(U16).rearrange("p (t q) -> p t q", t=PACK),
+                in_=w2_raw[:, H * b : H * (b + 1)].bitcast(U16).rearrange("p (q t) -> p t q", t=PACK),
+            )
+            nc.vector.tensor_copy(
+                out=w2_plane[:, KP * b : KP * (b + 1)].rearrange("p (t q) -> p t q", t=PACK),
+                in_=w2_plane_raw[:, KP * b : KP * (b + 1)].rearrange("p (q t) -> p t q", t=PACK),
+            )
+
         h2 = []
-        for s in range(SLICES):
+
+        def first_product_b(s):
             acc = bank(s)
             nc.tensor.matmul_mx(
                 out=acc[:],
@@ -177,9 +176,9 @@ def tile_list_tsunami_alert_scores_kernel(
         v_plane = held("v_plane", [P, S], U8)
 
         def gather_records():
+            nc.vector.tensor_copy(v_plane[:], tab_plane[:].indirect(list1[:]))
             for a in range(2):
                 nc.vector.tensor_copy(v_words[a][:], tab_sb[a][:].bitcast(U32).indirect(list1[:]))
-            nc.vector.tensor_copy(v_plane[:], tab_plane[:].indirect(list1[:]))
 
         def quantize(name, staged):
             codes = held(name + "_codes", [P, HALF], U32)
@@ -228,15 +227,25 @@ def tile_list_tsunami_alert_scores_kernel(
         w3_staged = {}
 
         def cast_w3(a):
-            raw = load_weight(w3, a, slice(0, N))
-            staged = stage_tile()
+            raw = w3_raw[a]
+            staged = held("w3_staged%d" % a, [P, PACK * HALF], BF16, tag=("tab2_sb", "w2_raw")[a])
             nc.scalar.copy(
                 out=staged[:].rearrange("p (c i j) -> p c j i", i=4, j=PACK),
                 in_=raw[:].rearrange("p j (c i) -> p c j i", i=4),
             )
             w3_staged[a] = staged
 
+        deal_w2(0)
+        for s in range(PACK):
+            first_product_b(s)
         scatter_b(0)
+        deal_w2(1)
+        for s in range(PACK, SLICES):
+            first_product_b(s)
+        for name, tag in (("pa1", "tab2_plane"), ("pa2", "w2_plane_raw")):
+            page = held(name, [P, T2], F32, tag=tag)
+            nc.vector.memset(page[:].bitcast(I32), 0)
+            pa_pages.append(page)
         scatter_b(1)
         max_b(0)
         gather_records()
@@ -258,9 +267,11 @@ def tile_list_tsunami_alert_scores_kernel(
 
         z = [held("z%d" % b, [P, 4, PACK, QUARTER], BF16) for b in range(2)]
 
-        def scatter_a(s):
+        def scatter_a(s, j0=0, j1=S):
             page = pa_pages[s % PA_PAGES]
-            nc.vector.tensor_tensor(page[:].indirect(list3[:]), h1[s][:], wg1_sb[:, s % PACK, :], ALU.mult)
+            nc.vector.tensor_tensor(
+                page[:].indirect(list3[:, j0 // 16 : j1 // 16]), h1[s][:, j0:j1], wg1_sb[:, s % PACK, j0:j1], ALU.mult
+            )
 
         def max_a(s, q0=0, q1=4):
             cols = slice(QUARTER * q0, QUARTER * q1)
@@ -308,32 +319,34 @@ def tile_list_tsunami_alert_scores_kernel(
             nc.vector.tensor_tensor(res[:], y2[:], res[:], ALU.add)
             nc.sync.dma_start(out=out[P * n : P * (n + 1), HALF * half : HALF * (half + 1)], in_=res[:])
 
+        for a in range(2):
+            w3_q[a] = quantize("w3_%d" % a, w3_staged[a])
         scatter_a(0)
         max_b(SLICES - 1)
-        for s in range(1, SLICES):
+        last = SLICES - 1
+        for s in range(1, last):
             scatter_a(s)
             max_a(s - 1)
-            if s == 2:
-                for a in range(2):
-                    w3_q[a] = quantize("w3_%d" % a, w3_staged[a])
             if s == PACK:
                 for q in range(4):
                     interleave(0, q, False)
-        last = SLICES - 1
+        max_a(last - 1)
+        scatter_a(last, 0, S // 2)
         quantize_z(0, 0)
+        scatter_a(last, S // 2, S)
         sums = [[bank(2 * n + which) for which in range(2)] for n in range(N // P)]
         for n in range(N // P):
             for which in range(2):
                 read_out_pass(sums[n][which], which, n, 0, 0)
         max_a(last, 0, 1)
-        interleave(1, 0, False)
         max_a(last, 1, 2)
+        interleave(1, 0, True)
+        interleave(1, 1, False)
         max_a(last, 2, 4)
-        interleave(1, 1, True)
         interleave(1, 2, False)
-        quantize_z(0, 1)
         quantize_z(1, 0)
         interleave(1, 3, True)
+        quantize_z(0, 1)
         for n in range(N // P):
             for which in range(2):
                 read_out_pass(sums[n][which], which, n, 1, 0)

@@ -66,24 +66,23 @@ def tile_list_tsunami_alert_scores_kernel(
             load(col[:], vec.rearrange("(b p t) -> p b t", b=2, t=PACK))
             return col
 
-        tab2_plane = held("tab2_plane", [P, T3], U8, tag="tab2_plane")
+        tab2_plane = held("tab2_plane", [P, T3], U8)
         w2_plane_raw = held("w2_plane_raw", [P, H], U8, tag="w2_plane_raw")
         tab_plane = held("tab_plane", [P, T], U8)
         w4_plane = held("w4_plane", [P, 2 * N], U8)
         pb_pages = [held("pb%d" % i, [P, T2], F32) for i in range(PB_PAGES)]
-        pa_pages = [held("pa0", [P, T2], F32)]
-        for plane in (tab2_plane, w2_plane_raw, tab_plane, w4_plane):
+        pa_pages = [held("pa%d" % i, [P, T2], F32) for i in range(PA_PAGES - 1)]
+        for plane in (tab2_plane, w2_plane_raw):
             nc.gpsimd.memset(plane[:].bitcast(I32), 0)
         for page in pb_pages + pa_pages:
             nc.vector.memset(page[:].bitcast(I32), 0)
 
         list2 = load_list("list2", offs2)
-        load_plane(tab2_plane, tab2_scales, (0, 1))
+        load_plane(tab2_plane, tab2_scales, range(4))
         w2_raw = held("w2_raw", [P, 2 * H], U8, tag="w2_raw")
         load(w2_raw[:].bitcast(I32), w2_words[0].bitcast(I32))
         tab2_sb = held("tab2_sb", [P, T3], I32, tag="tab2_sb")
         load(tab2_sb[:], tab2_words[0].rearrange("p t i -> p (t i)").bitcast(I32))
-        load_plane(tab2_plane, tab2_scales, (2, 3))
         load_plane(w2_plane_raw, w2_scales, range(4))
         list4 = load_list("list4", offs4)
         wg2_sb = load_dealt("wg2_sb", wg2)
@@ -110,36 +109,19 @@ def tile_list_tsunami_alert_scores_kernel(
         w1_raw[0, 1] = load_weight(w1, 0, slice(HALF, H))
         w1_raw[1, 1] = load_weight(w1, 1, slice(HALF, H))
         w3_raw = [load_weight(w3, a, slice(0, N)) for a in range(2)]
-        for q in range(4):
-            load(
-                w4_plane[32 * q : 32 * q + 4, :].bitcast(I32).rearrange("r (a c) -> r a c", a=2),
-                w4_scales[:, 4 * q : 4 * q + 4, :].rearrange("a r c -> r a c").bitcast(I32),
-            )
-        w4_sb = held("w4_sb", [P, 2, 2 * N], U8)
-        load(w4_sb[:].bitcast(I32), w4_words.rearrange("a p c -> p a c").bitcast(I32))
-        list1 = load_list("list1", offs)
-        for q in range(4):
-            load(tab_plane[32 * q : 32 * q + 8, :].bitcast(I32), tab_scales[:, 4 * q : 4 * q + 4, :].bitcast(I32))
-        tab_sb = [held("tab_sb%d" % a, [P, T], I32) for a in range(2)]
-        for a in range(2):
-            load(tab_sb[a][:], tab_words[a].rearrange("p t i -> p (t i)").bitcast(I32))
-        for s in range(5, SLICES):
-            load_tide(s)
-        list3 = load_list("list3", offs3)
-        wg1_sb = load_dealt("wg1_sb", wg1)
 
         v2_words = held("v2_words", [P, S], U32)
         v2_plane = held("v2_plane", [P, S], U8)
-        nc.vector.tensor_copy(v2_words[:], tab2_sb[:].bitcast(U32).indirect(list2[:]))
-        nc.vector.tensor_copy(v2_plane[:], tab2_plane[:].indirect(list2[:]))
         w2_sb = held("w2_sb", [P, 2 * H], U8)
         w2_plane = held("w2_plane", [P, H], U8)
 
-        def deal_w2(b):
+        def deal_w2_words(b):
             nc.vector.tensor_copy(
                 out=w2_sb[:, H * b : H * (b + 1)].bitcast(U16).rearrange("p (t q) -> p t q", t=PACK),
                 in_=w2_raw[:, H * b : H * (b + 1)].bitcast(U16).rearrange("p (q t) -> p t q", t=PACK),
             )
+
+        def deal_w2_scales(b):
             nc.vector.tensor_copy(
                 out=w2_plane[:, KP * b : KP * (b + 1)].rearrange("p (t q) -> p t q", t=PACK),
                 in_=w2_plane_raw[:, KP * b : KP * (b + 1)].rearrange("p (q t) -> p t q", t=PACK),
@@ -172,6 +154,7 @@ def tile_list_tsunami_alert_scores_kernel(
                 in1=tide_sb[s][:], op0=ALU.mult, op1=ALU.max,
             )
 
+        tab_sb = [held("tab_sb%d" % a, [P, T], I32) for a in range(2)]
         v_words = [held("v_words%d" % a, [P, S], U32) for a in range(2)]
         v_plane = held("v_plane", [P, S], U8)
 
@@ -235,17 +218,37 @@ def tile_list_tsunami_alert_scores_kernel(
             )
             w3_staged[a] = staged
 
-        deal_w2(0)
+        nc.vector.tensor_copy(v2_plane[:], tab2_plane[:].indirect(list2[:]))
+        deal_w2_words(0)
+        nc.vector.tensor_copy(v2_words[:], tab2_sb[:].bitcast(U32).indirect(list2[:]))
+        deal_w2_scales(0)
         for s in range(PACK):
             first_product_b(s)
         scatter_b(0)
-        deal_w2(1)
+        deal_w2_words(1)
+        deal_w2_scales(1)
         for s in range(PACK, SLICES):
             first_product_b(s)
-        for name, tag in (("pa1", "tab2_plane"), ("pa2", "w2_plane_raw")):
-            page = held(name, [P, T2], F32, tag=tag)
-            nc.vector.memset(page[:].bitcast(I32), 0)
-            pa_pages.append(page)
+        pa_pages.append(held("pa2", [P, T2], F32, tag="w2_plane_raw"))
+        nc.vector.memset(pa_pages[-1][:].bitcast(I32), 0)
+        for plane in (tab_plane, w4_plane):
+            nc.vector.memset(plane[:].bitcast(I32), 0)
+        for q in range(4):
+            load(
+                w4_plane[32 * q : 32 * q + 4, :].bitcast(I32).rearrange("r (a c) -> r a c", a=2),
+                w4_scales[:, 4 * q : 4 * q + 4, :].rearrange("a r c -> r a c").bitcast(I32),
+            )
+        w4_sb = held("w4_sb", [P, 2, 2 * N], U8)
+        load(w4_sb[:].bitcast(I32), w4_words.rearrange("a p c -> p a c").bitcast(I32))
+        list1 = load_list("list1", offs)
+        for q in range(4):
+            load(tab_plane[32 * q : 32 * q + 8, :].bitcast(I32), tab_scales[:, 4 * q : 4 * q + 4, :].bitcast(I32))
+        for a in range(2):
+            load(tab_sb[a][:], tab_words[a].rearrange("p t i -> p (t i)").bitcast(I32))
+        for s in range(5, SLICES):
+            load_tide(s)
+        list3 = load_list("list3", offs3)
+        wg1_sb = load_dealt("wg1_sb", wg1)
         scatter_b(1)
         max_b(0)
         gather_records()
@@ -300,7 +303,15 @@ def tile_list_tsunami_alert_scores_kernel(
         def quantize_z(b, half):
             z_q[b, half] = quantize("z_%d%d" % (b, half), z_staged[b, half])
 
-        def read_out_pass(acc, which, n, b, half):
+        def quantize_z_quarter(q):
+            codes, plane = z_q[1, 0]
+            cols = slice(QUARTER * q, QUARTER * (q + 1))
+            nc.vector.quantize_mx(
+                out=codes[:, cols].bitcast(FP8X4), scales=plane[:, cols],
+                in_=z_staged[1, 0][:, PACK * QUARTER * q : PACK * QUARTER * (q + 1)],
+            )
+
+        def read_out_pass(acc, which, n, b, half, cols, start, stop):
             codes, plane = z_q[b, half]
             if which == 0:
                 w_codes = w3_q[b][0][:, P * n : P * (n + 1)].bitcast(FP8X4)
@@ -309,15 +320,18 @@ def tile_list_tsunami_alert_scores_kernel(
                 w_codes = w4_sb[:, b, 2 * P * n : 2 * P * (n + 1)].bitcast(FP4X4)
                 w_plane = w4_plane[:, N * b + P * n : N * b + P * (n + 1)]
             nc.tensor.matmul_mx(
-                out=acc[:], lhsT=w_codes, lhsT_scale=w_plane, rhs=codes[:].bitcast(FP8X4), rhs_scale=plane[:],
-                start=(b == 0), stop=(b == 1),
+                out=acc[:, cols], lhsT=w_codes, lhsT_scale=w_plane, rhs=codes[:, cols].bitcast(FP8X4),
+                rhs_scale=plane[:, cols], start=start, stop=stop,
             )
 
-        def finish(y1, y2, n, half):
+        def bound(y1):
             res = rows.tile([P, HALF], F32, name="row")
             nc.scalar.activation(out=res[:], in_=y1[:], func=ACT.Tanh)
-            nc.vector.tensor_tensor(res[:], y2[:], res[:], ALU.add)
-            nc.sync.dma_start(out=out[P * n : P * (n + 1), HALF * half : HALF * (half + 1)], in_=res[:])
+            return res
+
+        def finish(res, y2, n, half, cols):
+            nc.vector.tensor_tensor(res[:, cols], y2[:, cols], res[:, cols], ALU.add)
+            nc.sync.dma_start(out=out[P * n : P * (n + 1), HALF * half : HALF * (half + 1)][:, cols], in_=res[:, cols])
 
         for a in range(2):
             w3_q[a] = quantize("w3_%d" % a, w3_staged[a])
@@ -334,28 +348,39 @@ def tile_list_tsunami_alert_scores_kernel(
         scatter_a(last, 0, S // 2)
         quantize_z(0, 0)
         scatter_a(last, S // 2, S)
+        whole = slice(0, HALF)
+        quarters = (slice(0, QUARTER), slice(QUARTER, HALF))
         sums = [[bank(2 * n + which) for which in range(2)] for n in range(N // P)]
         for n in range(N // P):
             for which in range(2):
-                read_out_pass(sums[n][which], which, n, 0, 0)
+                read_out_pass(sums[n][which], which, n, 0, 0, whole, True, False)
+        z_q[1, 0] = held("z_10_codes", [P, HALF], U32), held("z_10_plane", [P, HALF], U8)
         max_a(last, 0, 1)
         max_a(last, 1, 2)
         interleave(1, 0, True)
         interleave(1, 1, False)
-        max_a(last, 2, 4)
+        max_a(last, 2, 3)
         interleave(1, 2, False)
-        quantize_z(1, 0)
+        quantize_z_quarter(0)
+        max_a(last, 3, 4)
+        quantize_z_quarter(1)
         interleave(1, 3, True)
         quantize_z(0, 1)
-        for n in range(N // P):
-            for which in range(2):
-                read_out_pass(sums[n][which], which, n, 1, 0)
+        for q in range(2):
+            for n in range(N // P):
+                for which in range(2):
+                    read_out_pass(sums[n][which], which, n, 1, 0, quarters[q], False, q == 1)
         quantize_z(1, 1)
         for n in range(N // P):
-            finish(sums[n][0], sums[n][1], n, 0)
+            finish(bound(sums[n][0]), sums[n][1], n, 0, whole)
         for n in range(N // P):
-            pair = [bank(2 * n + which) for which in range(2)]
-            for which in range(2):
+            y1 = bank(2 * n)
+            for b in range(2):
+                read_out_pass(y1, 0, n, b, 1, whole, b == 0, b == 1)
+            res = bound(y1)
+            pieces = ((2 * n + 1, whole),) if n < N // P - 1 else ((2 * n + 1, quarters[0]), (0, quarters[1]))
+            for index, cols in pieces:
+                y2 = bank(index)
                 for b in range(2):
-                    read_out_pass(pair[which], which, n, b, 1)
-            finish(pair[0], pair[1], n, 1)
+                    read_out_pass(y2, 1, n, b, 1, cols, b == 0, b == 1)
+                finish(res, y2, n, 1, cols)

from contextlib import ExitStack

import concourse.mybir as mybir

K, K2, T, T3, S, T2, H, N = 1024, 512, 2048, 1024, 512, 1024, 1024, 512
FLOPS = 2 * (K * H * S + K2 * H * S + 2 * H * N * T2)

F32 = mybir.dt.float32
BF16 = mybir.dt.bfloat16
I32 = mybir.dt.int32
U32 = mybir.dt.uint32
U16 = mybir.dt.uint16
U8 = mybir.dt.uint8
FP8X4 = mybir.dt.float8_e4m3fn_x4
FP4X4 = mybir.dt.float4_e2m1fn_x4
ACT = mybir.ActivationFunctionType
ALU = mybir.AluOpType

P = 128
PACK = 4
KP = P * PACK
SLICES = H // P
HALF = 512
QUARTER = 256
PB_PAGES = 3
PA_PAGES = 3


def tile_list_tsunami_alert_scores_kernel(
    tc, tab_words, tab_scales, tab2_words, tab2_scales, offs, offs2, offs3, offs4, w1, b1, gn1,
    w2_words, w2_scales, gn2, wg1, wg2, tide, w3, w4_words, w4_scales, out,
):
    nc = tc.nc
    with ExitStack() as ctx:
        keep = ctx.enter_context(tc.tile_pool(name="keep", bufs=1))
        ring = ctx.enter_context(tc.tile_pool(name="ring", bufs=4))
        rows = ctx.enter_context(tc.tile_pool(name="rows", bufs=10))
        psum = ctx.enter_context(tc.psum_pool(name="psum", bufs=1))

        def held(name, shape, dtype, tag=""):
            return keep.tile(shape, dtype, name=name, tag=tag, align_bytes=64)

        def bank(i):
            return psum.tile([P, HALF], F32, name="bank%d" % i)

        def load(dst, src):
            nc.sync.dma_start(out=dst, in_=src)

        def load_list(name, src):
            lst = keep.tile([P, S // 16], U16, name=name)
            nc.sync.dma_start(lst[:], src)
            return lst

        def load_plane(plane, scales, quadrants):
            for q in quadrants:
                load(plane[32 * q : 32 * q + 4, :].bitcast(I32), scales[0, 4 * q : 4 * q + 4, :].bitcast(I32))

        def load_dealt(name, wg):
            dealt = held(name, [P, PACK, S], F32)
            for u in range(4):
                load(dealt[32 * u : 32 * u + 32], wg.rearrange("(q t) j -> q t j", t=PACK))
            return dealt

        def load_channels(name, vec):
            col = held(name, [P, 2, PACK], F32)
            load(col[:], vec.rearrange("(b p t) -> p b t", b=2, t=PACK))
            return col

        tab2_plane = held("tab2_plane", [P, T3], U8)
        w2_plane_raw = held("w2_plane_raw", [P, H], U8, tag="w2_plane_raw")
        tab_plane = held("tab_plane", [P, T], U8)
        w4_plane = held("w4_plane", [P, 2 * N], U8)
        pb_pages = [held("pb%d" % i, [P, T2], F32) for i in range(PB_PAGES)]
        pa_pages = [held("pa%d" % i, [P, T2], F32) for i in range(PA_PAGES - 1)]
        for plane in (tab2_plane, w2_plane_raw):
            nc.gpsimd.memset(plane[:].bitcast(I32), 0)
        for page in pb_pages + pa_pages:
            nc.vector.memset(page[:].bitcast(I32), 0)

        list2 = load_list("list2", offs2)
        load_plane(tab2_plane, tab2_scales, range(4))
        w2_raw = held("w2_raw", [P, 2 * H], U8, tag="w2_raw")
        load(w2_raw[:].bitcast(I32), w2_words[0].bitcast(I32))
        tab2_sb = held("tab2_sb", [P, T3], I32, tag="tab2_sb")
        load(tab2_sb[:], tab2_words[0].rearrange("p t i -> p (t i)").bitcast(I32))
        load_plane(w2_plane_raw, w2_scales, range(4))
        list4 = load_list("list4", offs4)
        wg2_sb = load_dealt("wg2_sb", wg2)
        gn2_sb = load_channels("gn2_sb", gn2)

        tide_rows = tide.rearrange("(b p t) m -> b t p m", b=2, t=PACK)
        tide_sb = [held("tide%d" % s, [P, T2], F32) for s in range(SLICES)]

        def load_tide(s):
            load(tide_sb[s][:], tide_rows[s // PACK, s % PACK])

        def load_weight(w, a, cols):
            raw = ring.tile([P, PACK, HALF], F32, name="raw")
            load(raw[:], w[KP * a : KP * (a + 1), cols].rearrange("(p j) c -> p j c", j=PACK))
            return raw

        for s in range(5):
            load_tide(s)
        b1_sb = load_channels("b1_sb", b1)
        gn1_sb = load_channels("gn1_sb", gn1)
        w1_raw = {}
        w1_raw[0, 0] = load_weight(w1, 0, slice(0, HALF))
        w1_raw[1, 0] = load_weight(w1, 1, slice(0, HALF))
        w1_raw[0, 1] = load_weight(w1, 0, slice(HALF, H))
        w1_raw[1, 1] = load_weight(w1, 1, slice(HALF, H))
        w3_raw = [load_weight(w3, a, slice(0, N)) for a in range(2)]

        v2_words = held("v2_words", [P, S], U32)
        v2_plane = held("v2_plane", [P, S], U8)
        w2_sb = held("w2_sb", [P, 2 * H], U8)
        w2_plane = held("w2_plane", [P, H], U8)

        def deal_w2_words(b):
            nc.vector.tensor_copy(
                out=w2_sb[:, H * b : H * (b + 1)].bitcast(U16).rearrange("p (t q) -> p t q", t=PACK),
                in_=w2_raw[:, H * b : H * (b + 1)].bitcast(U16).rearrange("p (q t) -> p t q", t=PACK),
            )

        def deal_w2_scales(b):
            nc.vector.tensor_copy(
                out=w2_plane[:, KP * b : KP * (b + 1)].rearrange("p (t q) -> p t q", t=PACK),
                in_=w2_plane_raw[:, KP * b : KP * (b + 1)].rearrange("p (q t) -> p t q", t=PACK),
            )

        h2 = []

        def first_product_b(s):
            acc = bank(s)
            nc.tensor.matmul_mx(
                out=acc[:],
                lhsT=w2_sb[:, 2 * P * s : 2 * P * (s + 1)].bitcast(FP4X4),
                lhsT_scale=w2_plane[:, P * s : P * (s + 1)],
                rhs=v2_words[:].bitcast(FP8X4),
                rhs_scale=v2_plane[:],
                start=True,
                stop=True,
            )
            h = rows.tile([P, S], F32, name="row")
            nc.scalar.activation(out=h[:], in_=acc[:], func=ACT.Silu)
            h2.append(h)

        def scatter_b(s):
            page = pb_pages[s % PB_PAGES]
            nc.vector.tensor_tensor(page[:].indirect(list4[:]), h2[s][:], wg2_sb[:, s % PACK, :], ALU.mult)

        def max_b(s):
            nc.vector.scalar_tensor_tensor(
                out=tide_sb[s][:], in0=pb_pages[s % PB_PAGES][:], scalar=gn2_sb[:, s // PACK, s % PACK : s % PACK + 1],
                in1=tide_sb[s][:], op0=ALU.mult, op1=ALU.max,
            )

        tab_sb = [held("tab_sb%d" % a, [P, T], I32) for a in range(2)]
        v_words = [held("v_words%d" % a, [P, S], U32) for a in range(2)]
        v_plane = held("v_plane", [P, S], U8)

        def gather_records():
            nc.vector.tensor_copy(v_plane[:], tab_plane[:].indirect(list1[:]))
            for a in range(2):
                nc.vector.tensor_copy(v_words[a][:], tab_sb[a][:].bitcast(U32).indirect(list1[:]))

        def quantize(name, staged):
            codes = held(name + "_codes", [P, HALF], U32)
            plane = held(name + "_plane", [P, HALF], U8)
            nc.vector.quantize_mx(out=codes[:].bitcast(FP8X4), scales=plane[:], in_=staged[:])
            return codes, plane

        def stage_tile():
            return ring.tile([P, PACK * HALF], BF16, name="staged", align_bytes=64)

        w1_staged = {}
        w1_q = {}

        def cast_w1(a, b):
            staged = stage_tile()
            nc.scalar.copy(
                out=staged[:].rearrange("p (t m j) -> p m j t", t=PACK, j=PACK),
                in_=w1_raw[a, b][:].rearrange("p j (m t) -> p m j t", t=PACK),
            )
            w1_staged[a, b] = staged

        def quantize_w1(a, b):
            w1_q[a, b] = quantize("w1_%d%d" % (a, b), w1_staged[a, b])

        h1 = []

        def first_product_a(b):
            for t in range(PACK):
                acc = bank(PACK * b + t)
                for a in range(2):
                    codes, plane = w1_q[a, b]
                    nc.tensor.matmul_mx(
                        out=acc[:],
                        lhsT=codes[:, P * t : P * (t + 1)].bitcast(FP8X4),
                        lhsT_scale=plane[:, P * t : P * (t + 1)],
                        rhs=v_words[a][:].bitcast(FP8X4),
                        rhs_scale=v_plane[4 * a :, :],
                        start=(a == 0),
                        stop=(a == 1),
                    )
                h = rows.tile([P, S], F32, name="row")
                nc.scalar.activation(out=h[:], in_=acc[:], func=ACT.Tanh, bias=b1_sb[:, b, t : t + 1])
                h1.append(h)

        w3_q = {}
        w3_staged = {}

        def cast_w3(a):
            raw = w3_raw[a]
            staged = held("w3_staged%d" % a, [P, PACK * HALF], BF16, tag=("tab2_sb", "w2_raw")[a])
            nc.scalar.copy(
                out=staged[:].rearrange("p (c i j) -> p c j i", i=4, j=PACK),
                in_=raw[:].rearrange("p j (c i) -> p c j i", i=4),
            )
            w3_staged[a] = staged

        nc.vector.tensor_copy(v2_plane[:], tab2_plane[:].indirect(list2[:]))
        deal_w2_words(0)
        nc.vector.tensor_copy(v2_words[:], tab2_sb[:].bitcast(U32).indirect(list2[:]))
        deal_w2_scales(0)
        for s in range(PACK):
            first_product_b(s)
        scatter_b(0)
        deal_w2_words(1)
        deal_w2_scales(1)
        for s in range(PACK, SLICES):
            first_product_b(s)
        pa_pages.append(held("pa2", [P, T2], F32, tag="w2_plane_raw"))
        nc.vector.memset(pa_pages[-1][:].bitcast(I32), 0)
        for plane in (tab_plane, w4_plane):
            nc.vector.memset(plane[:].bitcast(I32), 0)
        for q in range(4):
            load(
                w4_plane[32 * q : 32 * q + 4, :].bitcast(I32).rearrange("r (a c) -> r a c", a=2),
                w4_scales[:, 4 * q : 4 * q + 4, :].rearrange("a r c -> r a c").bitcast(I32),
            )
        w4_sb = held("w4_sb", [P, 2, 2 * N], U8)
        load(w4_sb[:].bitcast(I32), w4_words.rearrange("a p c -> p a c").bitcast(I32))
        list1 = load_list("list1", offs)
        for q in range(4):
            load(tab_plane[32 * q : 32 * q + 8, :].bitcast(I32), tab_scales[:, 4 * q : 4 * q + 4, :].bitcast(I32))
        for a in range(2):
            load(tab_sb[a][:], tab_words[a].rearrange("p t i -> p (t i)").bitcast(I32))
        for s in range(5, SLICES):
            load_tide(s)
        list3 = load_list("list3", offs3)
        wg1_sb = load_dealt("wg1_sb", wg1)
        scatter_b(1)
        max_b(0)
        gather_records()
        for a, b in ((0, 0), (1, 0), (0, 1), (1, 1)):
            cast_w1(a, b)
        for s in range(2, SLICES):
            scatter_b(s)
            max_b(s - 1)
            if s == 3:
                quantize_w1(0, 0)
                quantize_w1(1, 0)
                first_product_a(0)
            if s == 5:
                quantize_w1(0, 1)
                quantize_w1(1, 1)
                first_product_a(1)
        for a in range(2):
            cast_w3(a)

        z = [held("z%d" % b, [P, 4, PACK, QUARTER], BF16) for b in range(2)]

        def scatter_a(s, j0=0, j1=S):
            page = pa_pages[s % PA_PAGES]
            nc.vector.tensor_tensor(
                page[:].indirect(list3[:, j0 // 16 : j1 // 16]), h1[s][:, j0:j1], wg1_sb[:, s % PACK, j0:j1], ALU.mult
            )

        def max_a(s, q0=0, q1=4):
            cols = slice(QUARTER * q0, QUARTER * q1)
            nc.vector.scalar_tensor_tensor(
                out=z[s // PACK][:, q0:q1, s % PACK, :],
                in0=pa_pages[s % PA_PAGES][:, cols].rearrange("p (q c) -> p q c", c=QUARTER),
                scalar=gn1_sb[:, s // PACK, s % PACK : s % PACK + 1],
                in1=tide_sb[s][:, cols].rearrange("p (q c) -> p q c", c=QUARTER),
                op0=ALU.mult, op1=ALU.max,
            )

        z_staged = {}
        z_q = {}

        def interleave(b, q, on_vector):
            if q % 2 == 0:
                z_staged[b, q // 2] = stage_tile()
            dst = z_staged[b, q // 2][:, (q % 2) * PACK * QUARTER : (q % 2 + 1) * PACK * QUARTER]
            dst = dst.rearrange("p (c i t) -> p c t i", i=4, t=PACK)
            src = z[b][:, q, :, :].rearrange("p t (c i) -> p c t i", i=4)
            if on_vector:
                nc.vector.tensor_copy(out=dst, in_=src)
            else:
                nc.scalar.copy(out=dst, in_=src)

        def quantize_z(b, half):
            z_q[b, half] = quantize("z_%d%d" % (b, half), z_staged[b, half])

        def quantize_z_quarter(q):
            codes, plane = z_q[1, 0]
            cols = slice(QUARTER * q, QUARTER * (q + 1))
            nc.vector.quantize_mx(
                out=codes[:, cols].bitcast(FP8X4), scales=plane[:, cols],
                in_=z_staged[1, 0][:, PACK * QUARTER * q : PACK * QUARTER * (q + 1)],
            )

        def read_out_pass(acc, which, n, b, half, cols, start, stop):
            codes, plane = z_q[b, half]
            if which == 0:
                w_codes = w3_q[b][0][:, P * n : P * (n + 1)].bitcast(FP8X4)
                w_plane = w3_q[b][1][:, P * n : P * (n + 1)]
            else:
                w_codes = w4_sb[:, b, 2 * P * n : 2 * P * (n + 1)].bitcast(FP4X4)
                w_plane = w4_plane[:, N * b + P * n : N * b + P * (n + 1)]
            nc.tensor.matmul_mx(
                out=acc[:, cols], lhsT=w_codes, lhsT_scale=w_plane, rhs=codes[:, cols].bitcast(FP8X4),
                rhs_scale=plane[:, cols], start=start, stop=stop,
            )

        def bound(y1):
            res = rows.tile([P, HALF], F32, name="row")
            nc.scalar.activation(out=res[:], in_=y1[:], func=ACT.Tanh)
            return res

        def finish(res, y2, n, half, cols):
            nc.vector.tensor_tensor(res[:, cols], y2[:, cols], res[:, cols], ALU.add)
            nc.sync.dma_start(out=out[P * n : P * (n + 1), HALF * half : HALF * (half + 1)][:, cols], in_=res[:, cols])

        for a in range(2):
            w3_q[a] = quantize("w3_%d" % a, w3_staged[a])
        scatter_a(0)
        max_b(SLICES - 1)
        last = SLICES - 1
        for s in range(1, last):
            scatter_a(s)
            max_a(s - 1)
            if s == PACK:
                for q in range(4):
                    interleave(0, q, False)
        max_a(last - 1)
        scatter_a(last, 0, S // 2)
        quantize_z(0, 0)
        scatter_a(last, S // 2, S)
        whole = slice(0, HALF)
        quarters = (slice(0, QUARTER), slice(QUARTER, HALF))
        sums = [[bank(2 * n + which) for which in range(2)] for n in range(N // P)]
        for n in range(N // P):
            for which in range(2):
                read_out_pass(sums[n][which], which, n, 0, 0, whole, True, False)
        z_q[1, 0] = held("z_10_codes", [P, HALF], U32), held("z_10_plane", [P, HALF], U8)
        max_a(last, 0, 1)
        max_a(last, 1, 2)
        interleave(1, 0, True)
        interleave(1, 1, False)
        max_a(last, 2, 3)
        interleave(1, 2, False)
        quantize_z_quarter(0)
        max_a(last, 3, 4)
        quantize_z_quarter(1)
        interleave(1, 3, True)
        quantize_z(0, 1)
        for q in range(2):
            for n in range(N // P):
                for which in range(2):
                    read_out_pass(sums[n][which], which, n, 1, 0, quarters[q], False, q == 1)
        quantize_z(1, 1)
        for n in range(N // P):
            finish(bound(sums[n][0]), sums[n][1], n, 0, whole)
        for n in range(N // P):
            y1 = bank(2 * n)
            for b in range(2):
                read_out_pass(y1, 0, n, b, 1, whole, b == 0, b == 1)
            res = bound(y1)
            pieces = ((2 * n + 1, whole),) if n < N // P - 1 else ((2 * n + 1, quarters[0]), (0, quarters[1]))
            for index, cols in pieces:
                y2 = bank(index)
                for b in range(2):
                    read_out_pass(y2, 1, n, b, 1, cols, b == 0, b == 1)
                finish(res, y2, n, 1, cols)
